import numpy as np
import ml_dtypes


def mxq(x, axis, fmt="e4m3"):
    dtype, down = {"e4m3": (ml_dtypes.float8_e4m3fn, 7), "e5m2": (ml_dtypes.float8_e5m2, 14)}[fmt]
    v = np.moveaxis(np.asarray(x, np.float32).astype(ml_dtypes.bfloat16).astype(np.float64), axis, -1)
    blocks = v.reshape(v.shape[:-1] + (-1, 32))
    amax = np.abs(blocks).max(-1, keepdims=True)
    byte = np.maximum(np.where(amax > 0, np.frexp(amax)[1] - 1 + 127, 0) - down, 1)
    scale = np.exp2(byte - 127.0)
    codes = (blocks / scale).astype(np.float32).astype(dtype).astype(np.float64)
    return np.moveaxis((codes * scale).reshape(v.shape), -1, axis)


WIDE = False


def mx_kscale(k):
    if not WIDE:
        return np.ones(k)
    levels = np.array([10, -10, 5, -5, 0])
    if k % 512:
        return np.exp2(np.random.permutation(np.resize(levels, k // 32))).repeat(32)
    a = np.empty((k // 512, 16))
    for p in range(k // 512):
        a[p, :8] = np.random.permutation(np.resize(levels, 8))
        for g in range(8):
            far = levels[np.abs(levels - a[p, g]) >= 10]
            a[p, g + 8] = far[np.random.randint(len(far))]
    return np.exp2(a.ravel()).repeat(32)


def f64(x):
    return np.asarray(x).astype(np.float64)


def striped(idx):
    return np.tile(idx.reshape(-1, 16).T, (8, 1)).astype(np.uint16)


def unstriped(offs):
    return offs[:16].T.reshape(-1).astype(np.int64)


E2M1 = np.array([0.0, 0.5, 1.0, 1.5, 2.0, 3.0, 4.0, 6.0, -0.0, -0.5, -1.0, -1.5, -2.0, -3.0, -4.0, -6.0])


def pack_weight(w, fmt):
    k, n = w.shape
    w = f64(np.asarray(w, np.float32).astype(ml_dtypes.bfloat16)).reshape(k // 32, 32, n)
    amax = np.abs(w).max(1)
    if fmt == "e4m3":
        byte = np.frexp(amax)[1] - 1 + 127 - 7
    else:
        mant, ex = np.frexp(amax / 6.0)
        byte = np.where(mant > 0.5, ex, ex - 1) + 127
    byte = np.clip(np.where(amax > 0, byte, 1), 1, 254)
    scaled = (w * np.exp2(127.0 - byte)[:, None, :]).reshape(k, n).astype(np.float32)
    by_word = np.ascontiguousarray(scaled.reshape(k // 512, 128, 4, n).transpose(0, 1, 3, 2))
    if fmt == "e4m3":
        words = by_word.astype(ml_dtypes.float8_e4m3fn).view(np.uint8)
    else:
        c = by_word.astype(ml_dtypes.float4_e2m1fn).view(np.uint8) & 0xF
        words = (c[..., 0::2] | (c[..., 1::2] << 4)).reshape(k // 512, 128, 2 * n)
    return np.ascontiguousarray(words), np.ascontiguousarray(byte.astype(np.uint8).reshape(k // 512, 16, n))


def unpack_weight(words, scales, fmt):
    g, _, n = scales.shape
    words = np.ascontiguousarray(words).reshape(g, 128, n, -1)
    if fmt == "e4m3":
        vals = words.view(ml_dtypes.float8_e4m3fn).astype(np.float64)
    else:
        nib = np.empty((g, 128, n, 4), np.uint8)
        nib[..., 0::2] = words & 0xF
        nib[..., 1::2] = words >> 4
        vals = E2M1[nib]
    vals = vals * np.repeat(np.exp2(scales.astype(np.float64) - 127.0), 8, axis=1)[..., None]
    return vals.transpose(0, 1, 3, 2).reshape(g * 512, n)


def relu(v):
    return np.maximum(v, 0.0)


K, T, E, C, N = 1024, 1536, 4, 256, 128
K8 = 512


def by_expert(wq, xq):
    return np.concatenate([wq[e].T @ xq[:, e * C:(e + 1) * C] for e in range(E)], axis=1)


def setup_inputs():
    n = np.random.standard_normal
    s = mx_kscale(K)[:, None]
    w = n((E, K, N)) / np.sqrt(K) / s[None]
    w8 = [pack_weight(m[:K8], "e4m3") for m in w]
    w4 = [pack_weight(m[K8:], "e2m1") for m in w]
    return {
        "xT": (n((K, T)) * s).astype(np.float32),
        "xr": n((N, T)).astype(np.float32),
        "w8_words": np.stack([m[0] for m in w8]),
        "w8_scales": np.stack([m[1] for m in w8]),
        "w4_words": np.stack([m[0] for m in w4]),
        "w4_scales": np.stack([m[1] for m in w4]),
        "b": (0.3 * n((N, E))).astype(np.float32),
        "gate": np.tile(np.random.uniform(0.2, 1.0, E * C), (N, 1)).astype(np.float32),
        "offs": striped(np.random.permutation(T)[:E * C]),
    }


def reference(xT, xr, w8_words, w8_scales, w4_words, w4_scales, b, gate, offs):
    idx = unstriped(offs)
    w = np.stack([np.concatenate([unpack_weight(w8_words[e], w8_scales[e], "e4m3"), unpack_weight(w4_words[e], w4_scales[e], "e2m1")]) for e in range(E)])
    xq = mxq(f64(xT)[:, idx], 0, "e4m3")
    y = by_expert(w, xq)
    y = relu(y + np.repeat(f64(b), C, axis=1))
    out = f64(xr).copy()
    out[:, idx] += f64(gate) * y
    return out

@@ -1,0 +1,149 @@
+from contextlib import ExitStack
+
+import concourse.mybir as mybir
+
+F32 = mybir.dt.float32
+BF16 = mybir.dt.bfloat16
+I32 = mybir.dt.int32
+U32 = mybir.dt.uint32
+U16 = mybir.dt.uint16
+U8 = mybir.dt.uint8
+FP8X4 = mybir.dt.float8_e4m3fn_x4
+FP4X4 = mybir.dt.float4_e2m1fn_x4
+MULT = mybir.AluOpType.mult
+ADD = mybir.AluOpType.add
+COPY = mybir.ActivationFunctionType.Copy
+RELU = mybir.ActivationFunctionType.Relu
+
+P = 128
+K, T, E, C, N = 1024, 1536, 4, 256, 128
+PASS = 512
+FLOPS = 2 * E * C * K * N
+
+CHUNKS = (
+    (0, 0, 512, 288),
+    (0, 512, 512, 288),
+    (0, 1024, 512, 288),
+    (1, 0, 512, 288),
+    (1, 512, 512, 288),
+    (1, 1024, 256, 128),
+    (1, 1280, 256, 96),
+)
+
+
+def tile_moe_res_lin_relu_kernel(
+    tc, xT, xr, w8_words, w8_scales, w4_words, w4_scales, b, gate, offs, out
+):
+    nc = tc.nc
+    with ExitStack() as ctx:
+        keep = ctx.enter_context(tc.tile_pool(name="keep", bufs=1))
+        psum = ctx.enter_context(tc.psum_pool(name="psum", bufs=1))
+
+        offsets = keep.tile([P, E * C // 16], U16, name="offsets")
+        raws = [keep.tile([P, 4, w], F32, name=f"raw{i}", align_bytes=64) for i, (a, c0, w, s) in enumerate(CHUNKS)]
+        groups = [keep.tile([P, w, 4], BF16, name=f"grp{i}", align_bytes=64) for i, (a, c0, w, s) in enumerate(CHUNKS)]
+        words = [keep.tile([P, T], U32, name=f"words{a}", align_bytes=64) for a in range(2)]
+        planes = keep.tile([P, T], U8, name="planes", align_bytes=64)
+        slot_words = [keep.tile([P, E * C], U32, name=f"slot_words{a}", align_bytes=64) for a in range(2)]
+        slot_planes = keep.tile([P, E * C], U8, name="slot_planes", align_bytes=64)
+        w8 = keep.tile([P, E, 4 * N], U8, name="w8", align_bytes=64)
+        w4 = keep.tile([P, E, 2 * N], U8, name="w4", align_bytes=64)
+        w_planes = keep.tile([P, E, N], U8, name="w_planes", align_bytes=64)
+        bias = keep.tile([P, E], F32, name="bias")
+        gates = keep.tile([P, E * C], F32, name="gates")
+        resid = keep.tile([P, T], F32, name="resid")
+        ys = [keep.tile([P, C], F32, name=f"y{e}") for e in range(E)]
+        routed = keep.tile([P, T], F32, name="routed")
+        sums = [keep.tile([P, 512], F32, name=f"sum{i}") for i in range(T // 512)]
+        banks = [psum.tile([P, C], F32, name=f"bank{e}") for e in range(E)]
+
+        nc.vector.memset(w_planes[:].rearrange("p e n -> p (e n)").bitcast(I32), 0)
+        nc.gpsimd.memset(planes[:], 0)
+        nc.vector.memset(routed[:], 0.0)
+
+        for i, (a, c0, w, s) in enumerate(CHUNKS):
+            src = xT[PASS * a : PASS * (a + 1), c0 : c0 + w].rearrange("(p j) w -> p j w", j=4)
+            nc.sync.dma_start(raws[i][:], src)
+            if i == 0:
+                nc.sync.dma_start(offsets[:], offs)
+        nc.sync.dma_start(w8[:].bitcast(I32), w8_words.rearrange("e a p n t -> p (e a) (n t)").bitcast(I32))
+        nc.sync.dma_start(w4[:].bitcast(I32), w4_words.rearrange("e a p m -> p (e a) m").bitcast(I32))
+        for first, scales in ((4, w8_scales), (0, w4_scales)):
+            for q in range(4):
+                nc.gpsimd.dma_start(
+                    w_planes[32 * q + first : 32 * q + first + 4, :, :].bitcast(I32),
+                    scales[:, 0, 4 * q : 4 * q + 4, :].rearrange("e q n -> q e n").bitcast(I32),
+                )
+        nc.gpsimd.dma_start(bias[:], b)
+        nc.sync.dma_start(gates[:], gate)
+        nc.sync.dma_start(resid[:], xr)
+
+        def cast(i):
+            a, c0, w, s = CHUNKS[i]
+            nc.scalar.activation(groups[i][:, 0:s, :], raws[i][:, :, 0:s].rearrange("p j w -> p w j"), COPY)
+            nc.vector.tensor_copy(groups[i][:, s:w, :], raws[i][:, :, s:w].rearrange("p j w -> p w j"))
+
+        def quantise(i):
+            a, c0, w, s = CHUNKS[i]
+            first = 4 if a == 0 else 0
+            nc.vector.quantize_mx(
+                out=words[a][:, c0 : c0 + w].bitcast(FP8X4),
+                scales=planes[first:P, c0 : c0 + w],
+                in_=groups[i][:].rearrange("p w j -> p (w j)"),
+            )
+
+        def gather_words(a, lo, hi):
+            nc.vector.tensor_copy(slot_words[a][:, lo:hi], words[a][:].indirect(offsets[:, lo // 16 : hi // 16]))
+
+        def gather_planes(lo, hi):
+            nc.vector.tensor_copy(slot_planes[:, lo:hi], planes[:].indirect(offsets[:, lo // 16 : hi // 16]))
+
+        def multiply(e):
+            for h in range(C // 128):
+                cols = slice(e * C + h * 128, e * C + (h + 1) * 128)
+                acc = banks[e][:, h * 128 : (h + 1) * 128]
+                nc.tensor.matmul_mx(
+                    out=acc,
+                    lhsT=w8[:, e, :].bitcast(FP8X4),
+                    lhsT_scale=w_planes[4:P, e, :],
+                    rhs=slot_words[0][:, cols].bitcast(FP8X4),
+                    rhs_scale=slot_planes[4:P, cols],
+                    start=True,
+                    stop=False,
+                )
+                nc.tensor.matmul_mx(
+                    out=acc,
+                    lhsT=w4[:, e, :].bitcast(FP4X4),
+                    lhsT_scale=w_planes[:, e, :],
+                    rhs=slot_words[1][:, cols].bitcast(FP8X4),
+                    rhs_scale=slot_planes[:, cols],
+                    start=False,
+                    stop=True,
+                )
+            nc.scalar.activation(ys[e][:], banks[e][:], RELU, bias=bias[:, e : e + 1])
+
+        def scatter(e):
+            nc.vector.tensor_tensor(
+                routed[:].indirect(offsets[:, e * C // 16 : (e + 1) * C // 16]), ys[e][:], gates[:, e * C : (e + 1) * C], MULT
+            )
+
+        n = len(CHUNKS)
+        for i in range(n):
+            cast(i)
+            if i == 4:
+                gather_words(0, 0, E * C)
+            if i >= 1:
+                quantise(i - 1)
+        quantise(n - 1)
+        for e in range(E + 2):
+            if e < E:
+                gather_words(1, e * C, (e + 1) * C)
+                gather_planes(e * C, (e + 1) * C)
+                multiply(e)
+            if e >= 2:
+                scatter(e - 2)
+
+        for i in range(T // 512):
+            cols = slice(i * 512, (i + 1) * 512)
+            nc.vector.tensor_tensor(sums[i][:], routed[:, cols], resid[:, cols], ADD)
+            nc.sync.dma_start(out[:, cols], sums[i][:])

@@ -30,6 +30,8 @@ CHUNKS = (
     (1, 1280, 256, 96),
 )
 
+CUTS = ((0, 512), (512, 1024), (1024, 1536))
+
 
 def tile_moe_res_lin_relu_kernel(
     tc, xT, xr, w8_words, w8_scales, w4_words, w4_scales, b, gate, offs, out
@@ -52,29 +54,38 @@ def tile_moe_res_lin_relu_kernel(
         bias = keep.tile([P, E], F32, name="bias")
         gates = keep.tile([P, E * C], F32, name="gates")
         resid = keep.tile([P, T], F32, name="resid")
-        ys = [keep.tile([P, C], F32, name=f"y{e}") for e in range(E)]
+        ys = [keep.tile([P, 2 * C], F32, name=f"y{g}") for g in range(2)]
         routed = keep.tile([P, T], F32, name="routed")
-        sums = [keep.tile([P, 512], F32, name=f"sum{i}") for i in range(T // 512)]
+        sums = [keep.tile([P, hi - lo], F32, name=f"sum{i}") for i, (lo, hi) in enumerate(CUTS)]
         banks = [psum.tile([P, C], F32, name=f"bank{e}") for e in range(E)]
 
         nc.vector.memset(w_planes[:].rearrange("p e n -> p (e n)").bitcast(I32), 0)
         nc.gpsimd.memset(planes[:], 0)
         nc.vector.memset(routed[:], 0.0)
 
-        for i, (a, c0, w, s) in enumerate(CHUNKS):
+        def load_x(i):
+            a, c0, w, s = CHUNKS[i]
             src = xT[PASS * a : PASS * (a + 1), c0 : c0 + w].rearrange("(p j) w -> p j w", j=4)
             nc.sync.dma_start(raws[i][:], src)
-            if i == 0:
-                nc.sync.dma_start(offsets[:], offs)
-        nc.sync.dma_start(w8[:].bitcast(I32), w8_words.rearrange("e a p n t -> p (e a) (n t)").bitcast(I32))
-        nc.sync.dma_start(w4[:].bitcast(I32), w4_words.rearrange("e a p m -> p (e a) m").bitcast(I32))
-        for first, scales in ((4, w8_scales), (0, w4_scales)):
+
+        def load_planes(first, scales):
             for q in range(4):
-                nc.gpsimd.dma_start(
+                nc.sync.dma_start(
                     w_planes[32 * q + first : 32 * q + first + 4, :, :].bitcast(I32),
                     scales[:, 0, 4 * q : 4 * q + 4, :].rearrange("e q n -> q e n").bitcast(I32),
                 )
-        nc.gpsimd.dma_start(bias[:], b)
+
+        load_x(0)
+        load_planes(4, w8_scales)
+        load_x(1)
+        load_x(2)
+        nc.sync.dma_start(offsets[:], offs)
+        load_planes(0, w4_scales)
+        for i in range(3, len(CHUNKS)):
+            load_x(i)
+        nc.sync.dma_start(w8[:].bitcast(I32), w8_words.rearrange("e a p n t -> p (e a) (n t)").bitcast(I32))
+        nc.sync.dma_start(w4[:].bitcast(I32), w4_words.rearrange("e a p m -> p (e a) m").bitcast(I32))
+        nc.sync.dma_start(bias[:], b)
         nc.sync.dma_start(gates[:], gate)
         nc.sync.dma_start(resid[:], xr)
 
@@ -120,30 +131,28 @@ def tile_moe_res_lin_relu_kernel(
                     start=False,
                     stop=True,
                 )
-            nc.scalar.activation(ys[e][:], banks[e][:], RELU, bias=bias[:, e : e + 1])
-
-        def scatter(e):
-            nc.vector.tensor_tensor(
-                routed[:].indirect(offsets[:, e * C // 16 : (e + 1) * C // 16]), ys[e][:], gates[:, e * C : (e + 1) * C], MULT
-            )
+            nc.scalar.activation(ys[e // 2][:, (e % 2) * C : (e % 2 + 1) * C], banks[e][:], RELU, bias=bias[:, e : e + 1])
 
         n = len(CHUNKS)
         for i in range(n):
-            cast(i)
-            if i == 4:
+            if i == 3:
+                quantise(2)
                 gather_words(0, 0, E * C)
-            if i >= 1:
+            cast(i)
+            if i >= 1 and i != 3:
                 quantise(i - 1)
         quantise(n - 1)
-        for e in range(E + 2):
-            if e < E:
-                gather_words(1, e * C, (e + 1) * C)
-                gather_planes(e * C, (e + 1) * C)
+        for g in range(2):
+            gather_words(1, g * 512, (g + 1) * 512)
+            gather_planes(g * 512, (g + 1) * 512)
+            for e in (2 * g, 2 * g + 1):
                 multiply(e)
-            if e >= 2:
-                scatter(e - 2)
+        for g in range(2):
+            nc.vector.tensor_tensor(
+                routed[:].indirect(offsets[:, g * 32 : (g + 1) * 32]), ys[g][:], gates[:, g * 512 : (g + 1) * 512], MULT
+            )
 
-        for i in range(T // 512):
-            cols = slice(i * 512, (i + 1) * 512)
+        for i, (lo, hi) in enumerate(CUTS):
+            cols = slice(lo, hi)
             nc.vector.tensor_tensor(sums[i][:], routed[:, cols], resid[:, cols], ADD)
             nc.sync.dma_start(out[:, cols], sums[i][:])

@@ -21,13 +21,13 @@ PASS = 512
 FLOPS = 2 * E * C * K * N
 
 CHUNKS = (
-    (0, 0, 512, 288),
-    (0, 512, 512, 288),
-    (0, 1024, 512, 288),
-    (1, 0, 512, 288),
-    (1, 512, 512, 288),
+    (0, 0, 512, 160),
+    (0, 512, 512, 160),
+    (0, 1024, 512, 144),
+    (1, 0, 512, 512),
+    (1, 512, 512, 256),
     (1, 1024, 256, 128),
-    (1, 1280, 256, 96),
+    (1, 1280, 256, 64),
 )
 
 CUTS = ((0, 512), (512, 1024), (1024, 1536))
@@ -76,23 +76,29 @@ def tile_moe_res_lin_relu_kernel(
                 )
 
         load_x(0)
-        load_planes(4, w8_scales)
         load_x(1)
-        load_x(2)
         nc.sync.dma_start(offsets[:], offs)
-        load_planes(0, w4_scales)
-        for i in range(3, len(CHUNKS)):
+        for i in range(2, len(CHUNKS)):
             load_x(i)
         nc.sync.dma_start(w8[:].bitcast(I32), w8_words.rearrange("e a p n t -> p (e a) (n t)").bitcast(I32))
         nc.sync.dma_start(w4[:].bitcast(I32), w4_words.rearrange("e a p m -> p (e a) m").bitcast(I32))
         nc.sync.dma_start(bias[:], b)
+        load_planes(4, w8_scales)
+        load_planes(0, w4_scales)
         nc.sync.dma_start(gates[:], gate)
         nc.sync.dma_start(resid[:], xr)
 
         def cast(i):
             a, c0, w, s = CHUNKS[i]
-            nc.scalar.activation(groups[i][:, 0:s, :], raws[i][:, :, 0:s].rearrange("p j w -> p w j"), COPY)
-            nc.vector.tensor_copy(groups[i][:, s:w, :], raws[i][:, :, s:w].rearrange("p j w -> p w j"))
+            for engine_copy, lo, hi in ((scalar_copy, 0, s), (nc.vector.tensor_copy, s, w)):
+                if hi > lo:
+                    engine_copy(
+                        groups[i][:, lo:hi, :].rearrange("p (c i) j -> p c j i", i=4),
+                        raws[i][:, :, lo:hi].rearrange("p j (c i) -> p c j i", i=4),
+                    )
+
+        def scalar_copy(dst, src):
+            nc.scalar.activation(dst, src, COPY)
 
         def quantise(i):
             a, c0, w, s = CHUNKS[i]

from contextlib import ExitStack

import concourse.mybir as mybir

F32 = mybir.dt.float32
BF16 = mybir.dt.bfloat16
I32 = mybir.dt.int32
U32 = mybir.dt.uint32
U16 = mybir.dt.uint16
U8 = mybir.dt.uint8
FP8X4 = mybir.dt.float8_e4m3fn_x4
FP4X4 = mybir.dt.float4_e2m1fn_x4
MULT = mybir.AluOpType.mult
ADD = mybir.AluOpType.add
COPY = mybir.ActivationFunctionType.Copy
RELU = mybir.ActivationFunctionType.Relu

P = 128
K, T, E, C, N = 1024, 1536, 4, 256, 128
PASS = 512
FLOPS = 2 * E * C * K * N

CHUNKS = (
    (0, 0, 512, 160),
    (0, 512, 512, 160),
    (0, 1024, 512, 144),
    (1, 0, 512, 512),
    (1, 512, 512, 256),
    (1, 1024, 256, 128),
    (1, 1280, 256, 64),
)

CUTS = ((0, 512), (512, 1024), (1024, 1536))


def tile_moe_res_lin_relu_kernel(
    tc, xT, xr, w8_words, w8_scales, w4_words, w4_scales, b, gate, offs, out
):
    nc = tc.nc
    with ExitStack() as ctx:
        keep = ctx.enter_context(tc.tile_pool(name="keep", bufs=1))
        psum = ctx.enter_context(tc.psum_pool(name="psum", bufs=1))

        offsets = keep.tile([P, E * C // 16], U16, name="offsets")
        raws = [keep.tile([P, 4, w], F32, name=f"raw{i}", align_bytes=64) for i, (a, c0, w, s) in enumerate(CHUNKS)]
        groups = [keep.tile([P, w, 4], BF16, name=f"grp{i}", align_bytes=64) for i, (a, c0, w, s) in enumerate(CHUNKS)]
        words = [keep.tile([P, T], U32, name=f"words{a}", align_bytes=64) for a in range(2)]
        planes = keep.tile([P, T], U8, name="planes", align_bytes=64)
        slot_words = [keep.tile([P, E * C], U32, name=f"slot_words{a}", align_bytes=64) for a in range(2)]
        slot_planes = keep.tile([P, E * C], U8, name="slot_planes", align_bytes=64)
        w8 = keep.tile([P, E, 4 * N], U8, name="w8", align_bytes=64)
        w4 = keep.tile([P, E, 2 * N], U8, name="w4", align_bytes=64)
        w_planes = keep.tile([P, E, N], U8, name="w_planes", align_bytes=64)
        bias = keep.tile([P, E], F32, name="bias")
        gates = keep.tile([P, E * C], F32, name="gates")
        resid = keep.tile([P, T], F32, name="resid")
        ys = [keep.tile([P, 2 * C], F32, name=f"y{g}") for g in range(2)]
        routed = keep.tile([P, T], F32, name="routed")
        sums = [keep.tile([P, hi - lo], F32, name=f"sum{i}") for i, (lo, hi) in enumerate(CUTS)]
        banks = [psum.tile([P, C], F32, name=f"bank{e}") for e in range(E)]

        nc.vector.memset(w_planes[:].rearrange("p e n -> p (e n)").bitcast(I32), 0)
        nc.gpsimd.memset(planes[:], 0)
        nc.vector.memset(routed[:], 0.0)

        def load_x(i):
            a, c0, w, s = CHUNKS[i]
            src = xT[PASS * a : PASS * (a + 1), c0 : c0 + w].rearrange("(p j) w -> p j w", j=4)
            nc.sync.dma_start(raws[i][:], src)

        def load_planes(first, scales):
            for q in range(4):
                nc.sync.dma_start(
                    w_planes[32 * q + first : 32 * q + first + 4, :, :].bitcast(I32),
                    scales[:, 0, 4 * q : 4 * q + 4, :].rearrange("e q n -> q e n").bitcast(I32),
                )

        load_x(0)
        load_x(1)
        nc.sync.dma_start(offsets[:], offs)
        for i in range(2, len(CHUNKS)):
            load_x(i)
        nc.sync.dma_start(w8[:].bitcast(I32), w8_words.rearrange("e a p n t -> p (e a) (n t)").bitcast(I32))
        nc.sync.dma_start(w4[:].bitcast(I32), w4_words.rearrange("e a p m -> p (e a) m").bitcast(I32))
        nc.sync.dma_start(bias[:], b)
        load_planes(4, w8_scales)
        load_planes(0, w4_scales)
        nc.sync.dma_start(gates[:], gate)
        nc.sync.dma_start(resid[:], xr)

        def cast(i):
            a, c0, w, s = CHUNKS[i]
            for engine_copy, lo, hi in ((scalar_copy, 0, s), (nc.vector.tensor_copy, s, w)):
                if hi > lo:
                    engine_copy(
                        groups[i][:, lo:hi, :].rearrange("p (c i) j -> p c j i", i=4),
                        raws[i][:, :, lo:hi].rearrange("p j (c i) -> p c j i", i=4),
                    )

        def scalar_copy(dst, src):
            nc.scalar.activation(dst, src, COPY)

        def quantise(i):
            a, c0, w, s = CHUNKS[i]
            first = 4 if a == 0 else 0
            nc.vector.quantize_mx(
                out=words[a][:, c0 : c0 + w].bitcast(FP8X4),
                scales=planes[first:P, c0 : c0 + w],
                in_=groups[i][:].rearrange("p w j -> p (w j)"),
            )

        def gather_words(a, lo, hi):
            nc.vector.tensor_copy(slot_words[a][:, lo:hi], words[a][:].indirect(offsets[:, lo // 16 : hi // 16]))

        def gather_planes(lo, hi):
            nc.vector.tensor_copy(slot_planes[:, lo:hi], planes[:].indirect(offsets[:, lo // 16 : hi // 16]))

        def multiply(e):
            for h in range(C // 128):
                cols = slice(e * C + h * 128, e * C + (h + 1) * 128)
                acc = banks[e][:, h * 128 : (h + 1) * 128]
                nc.tensor.matmul_mx(
                    out=acc,
                    lhsT=w8[:, e, :].bitcast(FP8X4),
                    lhsT_scale=w_planes[4:P, e, :],
                    rhs=slot_words[0][:, cols].bitcast(FP8X4),
                    rhs_scale=slot_planes[4:P, cols],
                    start=True,
                    stop=False,
                )
                nc.tensor.matmul_mx(
                    out=acc,
                    lhsT=w4[:, e, :].bitcast(FP4X4),
                    lhsT_scale=w_planes[:, e, :],
                    rhs=slot_words[1][:, cols].bitcast(FP8X4),
                    rhs_scale=slot_planes[:, cols],
                    start=False,
                    stop=True,
                )
            nc.scalar.activation(ys[e // 2][:, (e % 2) * C : (e % 2 + 1) * C], banks[e][:], RELU, bias=bias[:, e : e + 1])

        n = len(CHUNKS)
        for i in range(n):
            if i == 3:
                quantise(2)
                gather_words(0, 0, E * C)
            cast(i)
            if i >= 1 and i != 3:
                quantise(i - 1)
        quantise(n - 1)
        for g in range(2):
            gather_words(1, g * 512, (g + 1) * 512)
            gather_planes(g * 512, (g + 1) * 512)
            for e in (2 * g, 2 * g + 1):
                multiply(e)
        for g in range(2):
            nc.vector.tensor_tensor(
                routed[:].indirect(offsets[:, g * 32 : (g + 1) * 32]), ys[g][:], gates[:, g * 512 : (g + 1) * 512], MULT
            )

        for i, (lo, hi) in enumerate(CUTS):
            cols = slice(lo, hi)
            nc.vector.tensor_tensor(sums[i][:], routed[:, cols], resid[:, cols], ADD)
            nc.sync.dma_start(out[:, cols], sums[i][:])
